import numpy as np
CORES = [0,11,22,25,36,47,50,61,64,75,86,89]
N = 12
def setup_inputs(rng):
    return {"x": rng.standard_normal((N, 128, 96), dtype=np.float32)}
def reference(x):
    b = 96 // N
    blocks = x.reshape(N, 128, N, b)
    return {"y": np.ascontiguousarray(blocks.transpose(2, 1, 0, 3)).reshape(N, 128, 96)}

@@ -1,0 +1,168 @@
+from concourse.bass import DstId, RemoteDMATransfer
+
+N = 12
+B = 96 // N
+GROUPS = 3
+SIZE = N // GROUPS
+W = SIZE * B
+HALVES = 2
+PER = SIZE // HALVES
+HC = PER * B
+RH = 128 // HALVES
+NP = N // 2
+SLOTS = 8
+RS = 128 // SLOTS
+
+SCRATCH = {
+    "piece": ("dram", [GROUPS, 128, HALVES, HC], "float32"),
+    "gath": ("dram", [NP, 128, HALVES, HC], "float32"),
+    "msg": ("dram", [HALVES, 128, SLOTS, HC], "float32"),
+    "land0": ("dram", [128, SLOTS, HC], "float32"),
+    "land1": ("dram", [128, SLOTS, HC], "float32"),
+}
+SEMAPHORES = ["ld", "sent", "a1", "hd0", "hd1", "go", "a2_0", "a2_1", "st", "gst"]
+
+
+def _plan(cores, topo):
+    n = len(cores)
+    chips = [topo.chip(c) for c in cores]
+    planes = []
+    for r in range(n):
+        for pl in planes:
+            if chips[r] == chips[pl[0]] or topo.same_plane(chips[pl[0]], chips[r]):
+                pl.append(r)
+                break
+        else:
+            planes.append([r])
+    hub_of = []
+    for pl in planes:
+        free = [r for r in pl if all(topo.may_write(cores[r], cores[d]) for d in range(n) if d != r)]
+        row = {}
+        for r in free:
+            row.setdefault(r // SIZE, r)
+        hub_of.append(row)
+    return planes, hub_of
+
+
+def _engines(mask):
+    return [1 << k for k in range(mask.bit_length()) if (mask >> k) & 1]
+
+
+def _common(src, dsts, cores, topo):
+    m = -1
+    for d in dsts:
+        m &= topo.mask(cores[src], cores[d])
+    return m
+
+
+def _hop1(r, cores, topo, planes, hub_of):
+    p = [r in pl for pl in planes].index(True)
+    outs = [(q, hub_of[p][q]) for q in range(GROUPS) if hub_of[p][q] != r]
+    eng = _engines(_common(r, [h for _, h in outs], cores, topo))
+    per = 1
+    while per * 2 * len(outs) <= len(eng):
+        per *= 2
+    res = []
+    for k, (q, h) in enumerate(outs):
+        m = 0
+        for e in eng[k * per:(k + 1) * per]:
+            m |= e
+        res.append((q, h, m, per))
+    return res
+
+
+def _half_dests(h, u):
+    q = h // SIZE
+    return [d for d in range(q * SIZE + u * PER, q * SIZE + (u + 1) * PER) if d != h]
+
+
+def rank_program(g, core, T, topo):
+    r = T.rank_of(core)
+    if r is None:
+        return
+    cores = list(T.cores)
+    planes, hub_of = _plan(cores, topo)
+    p = [r in pl for pl in planes].index(True)
+    i = planes[p].index(r)
+    q_me, dd = divmod(r, SIZE)
+    u_me, e_me = divmod(dd, PER)
+    land = [T.land0, T.land1]
+    a2 = [T.sem.a2_0, T.sem.a2_1]
+    hd = [T.sem.hd0, T.sem.hd1]
+    hub = hub_of[p][q_me] == r
+    queues = [g.sync, g.scalar]
+
+    loaded = 0
+    for q in sorted(range(GROUPS), key=lambda q: hub_of[p][q] == r):
+        for u in range(HALVES):
+            c0 = q * W + u * HC
+            if hub_of[p][q] == r:
+                out = T.gath[i, u * RH:(u + 1) * RH]
+            else:
+                out = T.piece[q, u * RH:(u + 1) * RH]
+            queues[u % 2].dma_start(out, T.x[:, c0:c0 + HC]).then_inc(T.sem.ld, 16)
+            loaded += 16
+
+    g.wait_ge(T.sem.ld, loaded)
+    sent = 0
+    trs = []
+    for q, h, m, per in _hop1(r, cores, topo, planes, hub_of):
+        rid, pid, _ = topo.addr(cores[h])
+        trs.append(RemoteDMATransfer(dst_ids=[DstId(rid=rid, pnc=pid)], dma_engine_mask=m, remote_sem=T.sem.a1,
+                                     src=T.piece[q], dst=T.gath[i]))
+        sent += per
+    g.remote_dma_fused(trs, local_sem=T.sem.sent)
+
+    gdone = 0
+    if hub:
+        qs = [q for q in range(GROUPS) if hub_of[p][q] != r]
+        g.dma_start(T.msg[:, NP * RS:128], T.piece[qs[0]:qs[-1] + 1:qs[-1] - qs[0]]).then_inc(T.sem.gst, 16)
+        gdone += 16
+        g.wait_ge(T.sem.gst, gdone)
+        gathered = 0
+        for s in planes[p]:
+            if s != r:
+                gathered += sum(per for _, h, _, per in _hop1(s, cores, topo, planes, hub_of) if h == r)
+        for u in range(HALVES):
+            qu = queues[u % 2]
+            qu.wait_ge(T.sem.a1, gathered)
+            qu.wait_ge(T.sem.ld, loaded)
+            qu.dma_start(T.msg[u, 0:NP * RS], T.gath[:, u * RH:(u + 1) * RH]).then_inc(hd[u], 16)
+        for u in sorted(range(HALVES), key=lambda u: -len(_half_dests(r, u))):
+            dests = _half_dests(r, u)
+            m = _common(r, dests, cores, topo)
+            ids = []
+            for d in dests:
+                rid, pid, _ = topo.addr(cores[d])
+                ids.append(DstId(rid=rid, pnc=pid))
+            g.wait_ge(hd[u], 16)
+            g.remote_dma_fused([RemoteDMATransfer(dst_ids=ids, dma_engine_mask=m, remote_sem=a2[p],
+                                                  srcs=[T.msg[u]], dsts=[land[p][:] for _ in dests])],
+                               local_sem=T.sem.sent)
+            sent += len(_engines(m))
+        g.sem_inc(T.sem.go, 1)
+
+    g.dma_start(T.y[:, r * B:(r + 1) * B], T.x[:, r * B:(r + 1) * B]).then_inc(T.sem.gst, 16)
+    gdone += 16
+
+    stored = 0
+    for pp in range(len(planes)):
+        qu = queues[pp % 2]
+        h = hub_of[pp][q_me]
+        if h == r:
+            qu.wait_ge(T.sem.go, 1)
+        else:
+            qu.wait_ge(a2[pp], len(_engines(_common(h, _half_dests(h, u_me), cores, topo))))
+        for j, s in enumerate(planes[pp]):
+            if s == r:
+                continue
+            if h == r:
+                src = T.gath[j, u_me * RH:(u_me + 1) * RH, :, e_me * B:(e_me + 1) * B]
+            else:
+                src = land[pp][j * RS:(j + 1) * RS, :, e_me * B:(e_me + 1) * B]
+            qu.dma_start(T.y[:, s * B:(s + 1) * B], src).then_inc(T.sem.st, 16)
+            stored += 16
+
+    g.wait_ge(T.sem.sent, sent)
+    g.wait_ge(T.sem.gst, gdone)
+    g.wait_ge(T.sem.st, stored)

@@ -20,7 +20,7 @@ SCRATCH = {
     "land0": ("dram", [128, SLOTS, HC], "float32"),
     "land1": ("dram", [128, SLOTS, HC], "float32"),
 }
-SEMAPHORES = ["ld", "sent", "a1", "hd0", "hd1", "go", "a2_0", "a2_1", "st", "gst"]
+SEMAPHORES = ["ld", "sent1", "sent2", "a1", "pad", "hd0", "hd1", "go", "a2_0", "a2_1", "st"]
 
 
 def _plan(cores, topo):
@@ -76,6 +76,10 @@ def _half_dests(h, u):
     return [d for d in range(q * SIZE + u * PER, q * SIZE + (u + 1) * PER) if d != h]
 
 
+def _send_order(h):
+    return sorted(range(HALVES), key=lambda u: -len(_half_dests(h, u)))
+
+
 def rank_program(g, core, T, topo):
     r = T.rank_of(core)
     if r is None:
@@ -104,21 +108,26 @@ def rank_program(g, core, T, topo):
             loaded += 16
 
     g.wait_ge(T.sem.ld, loaded)
-    sent = 0
+    sent1 = 0
     trs = []
     for q, h, m, per in _hop1(r, cores, topo, planes, hub_of):
         rid, pid, _ = topo.addr(cores[h])
         trs.append(RemoteDMATransfer(dst_ids=[DstId(rid=rid, pnc=pid)], dma_engine_mask=m, remote_sem=T.sem.a1,
                                      src=T.piece[q], dst=T.gath[i]))
-        sent += per
-    g.remote_dma_fused(trs, local_sem=T.sem.sent)
+        sent1 += per
+    g.remote_dma_fused(trs, local_sem=T.sem.sent1)
 
-    gdone = 0
+    stored = 0
+    g.scalar.wait_ge(T.sem.sent1, sent1)
+    g.scalar.dma_start(T.y[:, r * B:(r + 1) * B], T.x[:, r * B:(r + 1) * B]).then_inc(T.sem.st, 16)
+    stored += 16
+
+    sent2 = 0
     if hub:
         qs = [q for q in range(GROUPS) if hub_of[p][q] != r]
-        g.dma_start(T.msg[:, NP * RS:128], T.piece[qs[0]:qs[-1] + 1:qs[-1] - qs[0]]).then_inc(T.sem.gst, 16)
-        gdone += 16
-        g.wait_ge(T.sem.gst, gdone)
+        g.sync.wait_ge(T.sem.ld, loaded)
+        g.sync.wait_ge(T.sem.sent1, sent1)
+        g.sync.dma_start(T.msg[:, NP * RS:128], T.piece[qs[0]:qs[-1] + 1:qs[-1] - qs[0]]).then_inc(T.sem.pad, 16)
         gathered = 0
         for s in planes[p]:
             if s != r:
@@ -128,7 +137,8 @@ def rank_program(g, core, T, topo):
             qu.wait_ge(T.sem.a1, gathered)
             qu.wait_ge(T.sem.ld, loaded)
             qu.dma_start(T.msg[u, 0:NP * RS], T.gath[:, u * RH:(u + 1) * RH]).then_inc(hd[u], 16)
-        for u in sorted(range(HALVES), key=lambda u: -len(_half_dests(r, u))):
+        g.wait_ge(T.sem.pad, 16)
+        for u in _send_order(r):
             dests = _half_dests(r, u)
             m = _common(r, dests, cores, topo)
             ids = []
@@ -138,21 +148,22 @@ def rank_program(g, core, T, topo):
             g.wait_ge(hd[u], 16)
             g.remote_dma_fused([RemoteDMATransfer(dst_ids=ids, dma_engine_mask=m, remote_sem=a2[p],
                                                   srcs=[T.msg[u]], dsts=[land[p][:] for _ in dests])],
-                               local_sem=T.sem.sent)
-            sent += len(_engines(m))
+                               local_sem=T.sem.sent2)
+            sent2 += len(_engines(m))
         g.sem_inc(T.sem.go, 1)
 
-    g.dma_start(T.y[:, r * B:(r + 1) * B], T.x[:, r * B:(r + 1) * B]).then_inc(T.sem.gst, 16)
-    gdone += 16
-
-    stored = 0
+    due = []
     for pp in range(len(planes)):
-        qu = queues[pp % 2]
         h = hub_of[pp][q_me]
-        if h == r:
-            qu.wait_ge(T.sem.go, 1)
-        else:
-            qu.wait_ge(a2[pp], len(_engines(_common(h, _half_dests(h, u_me), cores, topo))))
+        due.append((0 if h == r else 1 + _send_order(h).index(u_me), pp))
+    k = 0
+    for _, pp in sorted(due):
+        h = hub_of[pp][q_me]
+        for qu in queues:
+            if h == r:
+                qu.wait_ge(T.sem.go, 1)
+            else:
+                qu.wait_ge(a2[pp], len(_engines(_common(h, _half_dests(h, u_me), cores, topo))))
         for j, s in enumerate(planes[pp]):
             if s == r:
                 continue
@@ -160,9 +171,11 @@ def rank_program(g, core, T, topo):
                 src = T.gath[j, u_me * RH:(u_me + 1) * RH, :, e_me * B:(e_me + 1) * B]
             else:
                 src = land[pp][j * RS:(j + 1) * RS, :, e_me * B:(e_me + 1) * B]
-            qu.dma_start(T.y[:, s * B:(s + 1) * B], src).then_inc(T.sem.st, 16)
+            queues[k % 2].dma_start(T.y[:, s * B:(s + 1) * B], src).then_inc(T.sem.st, 16)
+            k += 1
             stored += 16
 
-    g.wait_ge(T.sem.sent, sent)
-    g.wait_ge(T.sem.gst, gdone)
+    g.wait_ge(T.sem.sent1, sent1)
+    if sent2:
+        g.wait_ge(T.sem.sent2, sent2)
     g.wait_ge(T.sem.st, stored)

@@ -5,22 +5,20 @@ B = 96 // N
 GROUPS = 3
 SIZE = N // GROUPS
 W = SIZE * B
-HALVES = 2
-PER = SIZE // HALVES
-HC = PER * B
-RH = 128 // HALVES
+RC = 128 // SIZE
 NP = N // 2
 SLOTS = 8
+M = SLOTS * B
 RS = 128 // SLOTS
 
 SCRATCH = {
-    "piece": ("dram", [GROUPS, 128, HALVES, HC], "float32"),
-    "gath": ("dram", [NP, 128, HALVES, HC], "float32"),
-    "msg": ("dram", [HALVES, 128, SLOTS, HC], "float32"),
-    "land0": ("dram", [128, SLOTS, HC], "float32"),
-    "land1": ("dram", [128, SLOTS, HC], "float32"),
+    "piece": ("dram", [GROUPS, 128, W], "float32"),
+    "gath": ("dram", [NP, 128, W], "float32"),
+    "msg": ("dram", [SIZE, 128, M], "float32"),
+    "land0": ("dram", [128, M], "float32"),
+    "land1": ("dram", [128, M], "float32"),
 }
-SEMAPHORES = ["ld", "sent1", "sent2", "a1", "pad", "hd0", "hd1", "go", "a2_0", "a2_1", "st"]
+SEMAPHORES = ["ld", "sent1", "sent2", "a1", "pad", "hd", "go", "a2_0", "a2_1", "st"]
 
 
 def _plan(cores, topo):
@@ -48,36 +46,44 @@ def _engines(mask):
     return [1 << k for k in range(mask.bit_length()) if (mask >> k) & 1]
 
 
-def _common(src, dsts, cores, topo):
-    m = -1
+def _shares(src, dsts, cores, topo, first_double):
+    common = -1
     for d in dsts:
-        m &= topo.mask(cores[src], cores[d])
-    return m
-
-
-def _hop1(r, cores, topo, planes, hub_of):
-    p = [r in pl for pl in planes].index(True)
-    outs = [(q, hub_of[p][q]) for q in range(GROUPS) if hub_of[p][q] != r]
-    eng = _engines(_common(r, [h for _, h in outs], cores, topo))
+        common &= topo.mask(cores[src], cores[d])
+    eng = _engines(common)
     per = 1
-    while per * 2 * len(outs) <= len(eng):
+    while per * 2 * len(dsts) <= len(eng):
         per *= 2
+    counts = [per] * len(dsts)
+    if first_double and per * (len(dsts) + 1) <= len(eng):
+        counts[0] = 2 * per
     res = []
-    for k, (q, h) in enumerate(outs):
+    at = 0
+    for d, c in zip(dsts, counts):
         m = 0
-        for e in eng[k * per:(k + 1) * per]:
+        for e in eng[at:at + c]:
             m |= e
-        res.append((q, h, m, per))
+        at += c
+        res.append((d, m, c))
     return res
 
 
-def _half_dests(h, u):
+def _plane_of(r, planes):
+    return [r in pl for pl in planes].index(True)
+
+
+def _hop1(r, cores, topo, planes, hub_of):
+    row = hub_of[_plane_of(r, planes)]
+    return _shares(r, [row[q] for q in range(GROUPS) if row[q] != r], cores, topo, False)
+
+
+def _hop2(h, cores, topo, planes, hub_of):
     q = h // SIZE
-    return [d for d in range(q * SIZE + u * PER, q * SIZE + (u + 1) * PER) if d != h]
-
-
-def _send_order(h):
-    return sorted(range(HALVES), key=lambda u: -len(_half_dests(h, u)))
+    p = _plane_of(h, planes)
+    hubs = [row[q] for row in hub_of]
+    dests = [d for d in range(q * SIZE, (q + 1) * SIZE) if d != h]
+    dests.sort(key=lambda d: (_plane_of(d, planes) == p, d in hubs))
+    return _shares(h, dests, cores, topo, True)
 
 
 def rank_program(g, core, T, topo):
@@ -86,35 +92,37 @@ def rank_program(g, core, T, topo):
         return
     cores = list(T.cores)
     planes, hub_of = _plan(cores, topo)
-    p = [r in pl for pl in planes].index(True)
+    p = _plane_of(r, planes)
     i = planes[p].index(r)
-    q_me, dd = divmod(r, SIZE)
-    u_me, e_me = divmod(dd, PER)
+    q_me, col = divmod(r, SIZE)
     land = [T.land0, T.land1]
     a2 = [T.sem.a2_0, T.sem.a2_1]
-    hd = [T.sem.hd0, T.sem.hd1]
     hub = hub_of[p][q_me] == r
     queues = [g.sync, g.scalar]
 
     loaded = 0
+    k = 0
     for q in sorted(range(GROUPS), key=lambda q: hub_of[p][q] == r):
-        for u in range(HALVES):
-            c0 = q * W + u * HC
+        for e in range(SIZE):
+            d = q * SIZE + e
             if hub_of[p][q] == r:
-                out = T.gath[i, u * RH:(u + 1) * RH]
+                if d == r:
+                    continue
+                out = T.gath[i, e * RC:(e + 1) * RC, :]
             else:
-                out = T.piece[q, u * RH:(u + 1) * RH]
-            queues[u % 2].dma_start(out, T.x[:, c0:c0 + HC]).then_inc(T.sem.ld, 16)
+                out = T.piece[q, e * RC:(e + 1) * RC, :]
+            queues[k % 2].dma_start(out, T.x[:, d * B:(d + 1) * B]).then_inc(T.sem.ld, 16)
+            k += 1
             loaded += 16
 
     g.wait_ge(T.sem.ld, loaded)
     sent1 = 0
     trs = []
-    for q, h, m, per in _hop1(r, cores, topo, planes, hub_of):
+    for h, m, c in _hop1(r, cores, topo, planes, hub_of):
         rid, pid, _ = topo.addr(cores[h])
         trs.append(RemoteDMATransfer(dst_ids=[DstId(rid=rid, pnc=pid)], dma_engine_mask=m, remote_sem=T.sem.a1,
-                                     src=T.piece[q], dst=T.gath[i]))
-        sent1 += per
+                                     src=T.piece[h // SIZE], dst=T.gath[i]))
+        sent1 += c
     g.remote_dma_fused(trs, local_sem=T.sem.sent1)
 
     stored = 0
@@ -127,35 +135,34 @@ def rank_program(g, core, T, topo):
         qs = [q for q in range(GROUPS) if hub_of[p][q] != r]
         g.sync.wait_ge(T.sem.ld, loaded)
         g.sync.wait_ge(T.sem.sent1, sent1)
-        g.sync.dma_start(T.msg[:, NP * RS:128], T.piece[qs[0]:qs[-1] + 1:qs[-1] - qs[0]]).then_inc(T.sem.pad, 16)
+        g.sync.dma_start(T.msg[:, NP * RS:128, :], T.piece[qs[0]:qs[-1] + 1:qs[-1] - qs[0]]).then_inc(T.sem.pad, 16)
         gathered = 0
         for s in planes[p]:
             if s != r:
-                gathered += sum(per for _, h, _, per in _hop1(s, cores, topo, planes, hub_of) if h == r)
-        for u in range(HALVES):
-            qu = queues[u % 2]
+                gathered += sum(c for h, _, c in _hop1(s, cores, topo, planes, hub_of) if h == r)
+        for qu in queues:
             qu.wait_ge(T.sem.a1, gathered)
             qu.wait_ge(T.sem.ld, loaded)
-            qu.dma_start(T.msg[u, 0:NP * RS], T.gath[:, u * RH:(u + 1) * RH]).then_inc(hd[u], 16)
+        outs = _hop2(r, cores, topo, planes, hub_of)
+        regrouped = 0
+        for k, (d, _, _) in enumerate(outs):
+            e = d % SIZE
+            queues[k % 2].dma_start(T.msg[e, 0:NP * RS, :], T.gath[:, e * RC:(e + 1) * RC, :]).then_inc(T.sem.hd, 16)
+            regrouped += 16
         g.wait_ge(T.sem.pad, 16)
-        for u in _send_order(r):
-            dests = _half_dests(r, u)
-            m = _common(r, dests, cores, topo)
-            ids = []
-            for d in dests:
-                rid, pid, _ = topo.addr(cores[d])
-                ids.append(DstId(rid=rid, pnc=pid))
-            g.wait_ge(hd[u], 16)
-            g.remote_dma_fused([RemoteDMATransfer(dst_ids=ids, dma_engine_mask=m, remote_sem=a2[p],
-                                                  srcs=[T.msg[u]], dsts=[land[p][:] for _ in dests])],
-                               local_sem=T.sem.sent2)
-            sent2 += len(_engines(m))
+        g.wait_ge(T.sem.hd, regrouped)
+        trs = []
+        for d, m, c in outs:
+            rid, pid, _ = topo.addr(cores[d])
+            trs.append(RemoteDMATransfer(dst_ids=[DstId(rid=rid, pnc=pid)], dma_engine_mask=m, remote_sem=a2[p],
+                                         src=T.msg[d % SIZE], dst=land[p][:, :]))
+            sent2 += c
+        g.remote_dma_fused(trs, local_sem=T.sem.sent2)
         g.sem_inc(T.sem.go, 1)
 
     due = []
     for pp in range(len(planes)):
-        h = hub_of[pp][q_me]
-        due.append((0 if h == r else 1 + _send_order(h).index(u_me), pp))
+        due.append((0 if hub_of[pp][q_me] == r else 1 if pp == p else 2, pp))
     k = 0
     for _, pp in sorted(due):
         h = hub_of[pp][q_me]
@@ -163,14 +170,14 @@ def rank_program(g, core, T, topo):
             if h == r:
                 qu.wait_ge(T.sem.go, 1)
             else:
-                qu.wait_ge(a2[pp], len(_engines(_common(h, _half_dests(h, u_me), cores, topo))))
+                qu.wait_ge(a2[pp], sum(c for d, _, c in _hop2(h, cores, topo, planes, hub_of) if d == r))
         for j, s in enumerate(planes[pp]):
             if s == r:
                 continue
             if h == r:
-                src = T.gath[j, u_me * RH:(u_me + 1) * RH, :, e_me * B:(e_me + 1) * B]
+                src = T.gath[j, col * RC:(col + 1) * RC, :]
             else:
-                src = land[pp][j * RS:(j + 1) * RS, :, e_me * B:(e_me + 1) * B]
+                src = land[pp][j * RS:(j + 1) * RS, :]
             queues[k % 2].dma_start(T.y[:, s * B:(s + 1) * B], src).then_inc(T.sem.st, 16)
             k += 1
             stored += 16

@@ -18,7 +18,7 @@ SCRATCH = {
     "land0": ("dram", [128, M], "float32"),
     "land1": ("dram", [128, M], "float32"),
 }
-SEMAPHORES = ["ld", "sent1", "sent2", "a1", "pad", "hd", "go", "a2_0", "a2_1", "st"]
+SEMAPHORES = ["ld0", "ld1", "ld2", "sent1", "sent2", "a1", "pad", "hd", "go", "a2_0", "a2_1", "st"]
 
 
 def _plan(cores, topo):
@@ -72,9 +72,15 @@ def _plane_of(r, planes):
     return [r in pl for pl in planes].index(True)
 
 
+def _order(r):
+    return [(r // SIZE + 1 + k) % GROUPS for k in range(GROUPS)]
+
+
 def _hop1(r, cores, topo, planes, hub_of):
     row = hub_of[_plane_of(r, planes)]
-    return _shares(r, [row[q] for q in range(GROUPS) if row[q] != r], cores, topo, False)
+    outs = [row[q] for q in _order(r) if row[q] != r]
+    calls = [outs[:2]] + ([outs[2:]] if outs[2:] else [])
+    return [_shares(r, c, cores, topo, False) for c in calls]
 
 
 def _hop2(h, cores, topo, planes, hub_of):
@@ -100,9 +106,10 @@ def rank_program(g, core, T, topo):
     hub = hub_of[p][q_me] == r
     queues = [g.sync, g.scalar]
 
-    loaded = 0
+    ld = [T.sem.ld0, T.sem.ld1, T.sem.ld2]
+    loaded = [0] * GROUPS
     k = 0
-    for q in sorted(range(GROUPS), key=lambda q: hub_of[p][q] == r):
+    for n, q in enumerate(_order(r)):
         for e in range(SIZE):
             d = q * SIZE + e
             if hub_of[p][q] == r:
@@ -111,19 +118,22 @@ def rank_program(g, core, T, topo):
                 out = T.gath[i, e * RC:(e + 1) * RC, :]
             else:
                 out = T.piece[q, e * RC:(e + 1) * RC, :]
-            queues[k % 2].dma_start(out, T.x[:, d * B:(d + 1) * B]).then_inc(T.sem.ld, 16)
+            queues[k % 2].dma_start(out, T.x[:, d * B:(d + 1) * B]).then_inc(ld[n], 16)
             k += 1
-            loaded += 16
+            loaded[n] += 16
 
-    g.wait_ge(T.sem.ld, loaded)
     sent1 = 0
-    trs = []
-    for h, m, c in _hop1(r, cores, topo, planes, hub_of):
-        rid, pid, _ = topo.addr(cores[h])
-        trs.append(RemoteDMATransfer(dst_ids=[DstId(rid=rid, pnc=pid)], dma_engine_mask=m, remote_sem=T.sem.a1,
-                                     src=T.piece[h // SIZE], dst=T.gath[i]))
-        sent1 += c
-    g.remote_dma_fused(trs, local_sem=T.sem.sent1)
+    n = 0
+    for call in _hop1(r, cores, topo, planes, hub_of):
+        trs = []
+        for h, m, c in call:
+            g.wait_ge(ld[n], loaded[n])
+            n += 1
+            rid, pid, _ = topo.addr(cores[h])
+            trs.append(RemoteDMATransfer(dst_ids=[DstId(rid=rid, pnc=pid)], dma_engine_mask=m, remote_sem=T.sem.a1,
+                                         src=T.piece[h // SIZE], dst=T.gath[i]))
+            sent1 += c
+        g.remote_dma_fused(trs, local_sem=T.sem.sent1)
 
     stored = 0
     g.scalar.wait_ge(T.sem.sent1, sent1)
@@ -133,16 +143,17 @@ def rank_program(g, core, T, topo):
     sent2 = 0
     if hub:
         qs = [q for q in range(GROUPS) if hub_of[p][q] != r]
-        g.sync.wait_ge(T.sem.ld, loaded)
+        for n in range(len(qs)):
+            g.sync.wait_ge(ld[n], loaded[n])
         g.sync.wait_ge(T.sem.sent1, sent1)
         g.sync.dma_start(T.msg[:, NP * RS:128, :], T.piece[qs[0]:qs[-1] + 1:qs[-1] - qs[0]]).then_inc(T.sem.pad, 16)
         gathered = 0
         for s in planes[p]:
             if s != r:
-                gathered += sum(c for h, _, c in _hop1(s, cores, topo, planes, hub_of) if h == r)
+                gathered += sum(c for call in _hop1(s, cores, topo, planes, hub_of) for h, _, c in call if h == r)
         for qu in queues:
             qu.wait_ge(T.sem.a1, gathered)
-            qu.wait_ge(T.sem.ld, loaded)
+            qu.wait_ge(ld[GROUPS - 1], loaded[GROUPS - 1])
         outs = _hop2(r, cores, topo, planes, hub_of)
         regrouped = 0
         for k, (d, _, _) in enumerate(outs):

from concourse.bass import DstId, RemoteDMATransfer

N = 12
B = 96 // N
GROUPS = 3
SIZE = N // GROUPS
W = SIZE * B
RC = 128 // SIZE
NP = N // 2
SLOTS = 8
M = SLOTS * B
RS = 128 // SLOTS

SCRATCH = {
    "piece": ("dram", [GROUPS, 128, W], "float32"),
    "gath": ("dram", [NP, 128, W], "float32"),
    "msg": ("dram", [SIZE, 128, M], "float32"),
    "land0": ("dram", [128, M], "float32"),
    "land1": ("dram", [128, M], "float32"),
}
SEMAPHORES = ["ld0", "ld1", "ld2", "sent1", "sent2", "a1", "pad", "hd", "go", "a2_0", "a2_1", "st"]


def _plan(cores, topo):
    n = len(cores)
    chips = [topo.chip(c) for c in cores]
    planes = []
    for r in range(n):
        for pl in planes:
            if chips[r] == chips[pl[0]] or topo.same_plane(chips[pl[0]], chips[r]):
                pl.append(r)
                break
        else:
            planes.append([r])
    hub_of = []
    for pl in planes:
        free = [r for r in pl if all(topo.may_write(cores[r], cores[d]) for d in range(n) if d != r)]
        row = {}
        for r in free:
            row.setdefault(r // SIZE, r)
        hub_of.append(row)
    return planes, hub_of


def _engines(mask):
    return [1 << k for k in range(mask.bit_length()) if (mask >> k) & 1]


def _shares(src, dsts, cores, topo, first_double):
    common = -1
    for d in dsts:
        common &= topo.mask(cores[src], cores[d])
    eng = _engines(common)
    per = 1
    while per * 2 * len(dsts) <= len(eng):
        per *= 2
    counts = [per] * len(dsts)
    if first_double and per * (len(dsts) + 1) <= len(eng):
        counts[0] = 2 * per
    res = []
    at = 0
    for d, c in zip(dsts, counts):
        m = 0
        for e in eng[at:at + c]:
            m |= e
        at += c
        res.append((d, m, c))
    return res


def _plane_of(r, planes):
    return [r in pl for pl in planes].index(True)


def _order(r):
    return [(r // SIZE + 1 + k) % GROUPS for k in range(GROUPS)]


def _hop1(r, cores, topo, planes, hub_of):
    row = hub_of[_plane_of(r, planes)]
    outs = [row[q] for q in _order(r) if row[q] != r]
    calls = [outs[:2]] + ([outs[2:]] if outs[2:] else [])
    return [_shares(r, c, cores, topo, False) for c in calls]


def _hop2(h, cores, topo, planes, hub_of):
    q = h // SIZE
    p = _plane_of(h, planes)
    hubs = [row[q] for row in hub_of]
    dests = [d for d in range(q * SIZE, (q + 1) * SIZE) if d != h]
    dests.sort(key=lambda d: (_plane_of(d, planes) == p, d in hubs))
    return _shares(h, dests, cores, topo, True)


def rank_program(g, core, T, topo):
    r = T.rank_of(core)
    if r is None:
        return
    cores = list(T.cores)
    planes, hub_of = _plan(cores, topo)
    p = _plane_of(r, planes)
    i = planes[p].index(r)
    q_me, col = divmod(r, SIZE)
    land = [T.land0, T.land1]
    a2 = [T.sem.a2_0, T.sem.a2_1]
    hub = hub_of[p][q_me] == r
    queues = [g.sync, g.scalar]

    ld = [T.sem.ld0, T.sem.ld1, T.sem.ld2]
    loaded = [0] * GROUPS
    k = 0
    for n, q in enumerate(_order(r)):
        for e in range(SIZE):
            d = q * SIZE + e
            if hub_of[p][q] == r:
                if d == r:
                    continue
                out = T.gath[i, e * RC:(e + 1) * RC, :]
            else:
                out = T.piece[q, e * RC:(e + 1) * RC, :]
            queues[k % 2].dma_start(out, T.x[:, d * B:(d + 1) * B]).then_inc(ld[n], 16)
            k += 1
            loaded[n] += 16

    sent1 = 0
    n = 0
    for call in _hop1(r, cores, topo, planes, hub_of):
        trs = []
        for h, m, c in call:
            g.wait_ge(ld[n], loaded[n])
            n += 1
            rid, pid, _ = topo.addr(cores[h])
            trs.append(RemoteDMATransfer(dst_ids=[DstId(rid=rid, pnc=pid)], dma_engine_mask=m, remote_sem=T.sem.a1,
                                         src=T.piece[h // SIZE], dst=T.gath[i]))
            sent1 += c
        g.remote_dma_fused(trs, local_sem=T.sem.sent1)

    stored = 0
    g.scalar.wait_ge(T.sem.sent1, sent1)
    g.scalar.dma_start(T.y[:, r * B:(r + 1) * B], T.x[:, r * B:(r + 1) * B]).then_inc(T.sem.st, 16)
    stored += 16

    sent2 = 0
    if hub:
        qs = [q for q in range(GROUPS) if hub_of[p][q] != r]
        for n in range(len(qs)):
            g.sync.wait_ge(ld[n], loaded[n])
        g.sync.wait_ge(T.sem.sent1, sent1)
        g.sync.dma_start(T.msg[:, NP * RS:128, :], T.piece[qs[0]:qs[-1] + 1:qs[-1] - qs[0]]).then_inc(T.sem.pad, 16)
        gathered = 0
        for s in planes[p]:
            if s != r:
                gathered += sum(c for call in _hop1(s, cores, topo, planes, hub_of) for h, _, c in call if h == r)
        for qu in queues:
            qu.wait_ge(T.sem.a1, gathered)
            qu.wait_ge(ld[GROUPS - 1], loaded[GROUPS - 1])
        outs = _hop2(r, cores, topo, planes, hub_of)
        regrouped = 0
        for k, (d, _, _) in enumerate(outs):
            e = d % SIZE
            queues[k % 2].dma_start(T.msg[e, 0:NP * RS, :], T.gath[:, e * RC:(e + 1) * RC, :]).then_inc(T.sem.hd, 16)
            regrouped += 16
        g.wait_ge(T.sem.pad, 16)
        g.wait_ge(T.sem.hd, regrouped)
        trs = []
        for d, m, c in outs:
            rid, pid, _ = topo.addr(cores[d])
            trs.append(RemoteDMATransfer(dst_ids=[DstId(rid=rid, pnc=pid)], dma_engine_mask=m, remote_sem=a2[p],
                                         src=T.msg[d % SIZE], dst=land[p][:, :]))
            sent2 += c
        g.remote_dma_fused(trs, local_sem=T.sem.sent2)
        g.sem_inc(T.sem.go, 1)

    due = []
    for pp in range(len(planes)):
        due.append((0 if hub_of[pp][q_me] == r else 1 if pp == p else 2, pp))
    k = 0
    for _, pp in sorted(due):
        h = hub_of[pp][q_me]
        for qu in queues:
            if h == r:
                qu.wait_ge(T.sem.go, 1)
            else:
                qu.wait_ge(a2[pp], sum(c for d, _, c in _hop2(h, cores, topo, planes, hub_of) if d == r))
        for j, s in enumerate(planes[pp]):
            if s == r:
                continue
            if h == r:
                src = T.gath[j, col * RC:(col + 1) * RC, :]
            else:
                src = land[pp][j * RS:(j + 1) * RS, :]
            queues[k % 2].dma_start(T.y[:, s * B:(s + 1) * B], src).then_inc(T.sem.st, 16)
            k += 1
            stored += 16

    g.wait_ge(T.sem.sent1, sent1)
    if sent2:
        g.wait_ge(T.sem.sent2, sent2)
    g.wait_ge(T.sem.st, stored)
